import numpy as np
import ml_dtypes


def mxq(x, axis, fmt="e4m3"):
    dtype, down = {"e4m3": (ml_dtypes.float8_e4m3fn, 7), "e5m2": (ml_dtypes.float8_e5m2, 14)}[fmt]
    v = np.moveaxis(np.asarray(x, np.float32).astype(ml_dtypes.bfloat16).astype(np.float64), axis, -1)
    blocks = v.reshape(v.shape[:-1] + (-1, 32))
    amax = np.abs(blocks).max(-1, keepdims=True)
    byte = np.maximum(np.where(amax > 0, np.frexp(amax)[1] - 1 + 127, 0) - down, 1)
    scale = np.exp2(byte - 127.0)
    codes = (blocks / scale).astype(np.float32).astype(dtype).astype(np.float64)
    return np.moveaxis((codes * scale).reshape(v.shape), -1, axis)


WIDE = False


def mx_kscale(k):
    if not WIDE:
        return np.ones(k)
    levels = np.array([10, -10, 5, -5, 0])
    if k % 512:
        return np.exp2(np.random.permutation(np.resize(levels, k // 32))).repeat(32)
    a = np.empty((k // 512, 16))
    for p in range(k // 512):
        a[p, :8] = np.random.permutation(np.resize(levels, 8))
        for g in range(8):
            far = levels[np.abs(levels - a[p, g]) >= 10]
            a[p, g + 8] = far[np.random.randint(len(far))]
    return np.exp2(a.ravel()).repeat(32)


def f64(x):
    return np.asarray(x).astype(np.float64)


def striped(idx):
    return np.tile(np.asarray(idx).reshape(-1, 16).T, (8, 1)).astype(np.uint16)


def unstriped(offs):
    return offs[:16].T.reshape(-1).astype(np.int64)


E2M1 = np.array([0.0, 0.5, 1.0, 1.5, 2.0, 3.0, 4.0, 6.0, -0.0, -0.5, -1.0, -1.5, -2.0, -3.0, -4.0, -6.0])


def pack_weight(w, fmt):
    k, n = w.shape
    w = f64(np.asarray(w, np.float32).astype(ml_dtypes.bfloat16)).reshape(k // 32, 32, n)
    amax = np.abs(w).max(1)
    if fmt == "e4m3":
        byte = np.frexp(amax)[1] - 1 + 127 - 7
    else:
        mant, ex = np.frexp(amax / 6.0)
        byte = np.where(mant > 0.5, ex, ex - 1) + 127
    byte = np.clip(np.where(amax > 0, byte, 1), 1, 254)
    scaled = (w * np.exp2(127.0 - byte)[:, None, :]).reshape(k, n).astype(np.float32)
    by_word = np.ascontiguousarray(scaled.reshape(k // 512, 128, 4, n).transpose(0, 1, 3, 2))
    if fmt == "e4m3":
        words = by_word.astype(ml_dtypes.float8_e4m3fn).view(np.uint8)
    else:
        c = by_word.astype(ml_dtypes.float4_e2m1fn).view(np.uint8) & 0xF
        words = (c[..., 0::2] | (c[..., 1::2] << 4)).reshape(k // 512, 128, 2 * n)
    return np.ascontiguousarray(words), np.ascontiguousarray(byte.astype(np.uint8).reshape(k // 512, 16, n))


def unpack_weight(words, scales, fmt):
    g, _, n = scales.shape
    words = np.ascontiguousarray(words).reshape(g, 128, n, -1)
    if fmt == "e4m3":
        vals = words.view(ml_dtypes.float8_e4m3fn).astype(np.float64)
    else:
        nib = np.empty((g, 128, n, 4), np.uint8)
        nib[..., 0::2] = words & 0xF
        nib[..., 1::2] = words >> 4
        vals = E2M1[nib]
    vals = vals * np.repeat(np.exp2(scales.astype(np.float64) - 127.0), 8, axis=1)[..., None]
    return vals.transpose(0, 1, 3, 2).reshape(g * 512, n)


def sigmoid(v):
    return 1.0 / (1.0 + np.exp(-v))


D, E, T, I, Q, G = 512, 512, 2048, 512, 128, 32


def setup_inputs():
    n = np.random.standard_normal
    idx = np.random.permutation(T)[:I]
    fd = mx_kscale(D)
    fe = mx_kscale(E)
    keysp = pack_weight(n((D, T)) / fd[:, None], "e2m1")
    valsp = pack_weight(n((E, T)) / fe[:, None], "e2m1")
    return {
        "query": (n((D, Q)) * 0.8 / np.sqrt(D) * fd[:, None]).astype(np.float32),
        "keys_words": keysp[0],
        "keys_scales": keysp[1],
        "th": (np.random.uniform(-0.5, 0.5, (Q, 1))).astype(np.float32),
        "sharp": (np.random.uniform(1.0, 3.0, (Q, 1))).astype(np.float32),
        "gout": (n((E, Q)) * 1 / np.sqrt(E) * fe[:, None]).astype(np.float32),
        "vals_words": valsp[0],
        "vals_scales": valsp[1],
        "old": (0.5 * n((Q, T))).astype(np.float32),
        "offs": striped(idx),
    }


def reference(query, keys_words, keys_scales, th, sharp, gout, vals_words, vals_scales, old, offs):
    idx = unstriped(offs)
    keysu = unpack_weight(keys_words, keys_scales, "e2m1")
    valsu = unpack_weight(vals_words, vals_scales, "e2m1")
    queryq = mxq(f64(query), 0, "e4m3")
    keysidxg = keysu[:, idx]
    a = queryq.T @ keysidxg
    s = a.reshape(Q, G, I // G).mean(axis=2) * f64(sharp)
    p = np.exp(s - np.max(s, axis=1, keepdims=True))
    z = np.sum(p, axis=1, keepdims=True)
    r = p / z
    rr = np.repeat(r, I // G, axis=1)
    goutq = mxq(f64(gout), 0, "e4m3")
    valsidxg = valsu[:, idx]
    c0 = goutq.T @ valsidxg
    drr = c0 * sigmoid(a - f64(th))
    dr = drr.reshape(Q, G, I // G).sum(axis=2)
    dz = np.sum(dr * p / np.square(z) * (-1.0), axis=1, keepdims=True)
    dp = dr / z + dz
    ds = dp * p
    e1 = ds * f64(sharp) / 16.0
    r1 = np.repeat(e1, I // G, axis=1)
    da = c0 * rr * sigmoid(a - f64(th)) * (1.0 - sigmoid(a - f64(th))) + r1
    gs = da * 32.0
    gf = np.zeros((Q, T))
    gf[:, idx] = gs
    y = f64(old) + gf
    return y

@@ -1,0 +1,193 @@
+import math
+from contextlib import ExitStack
+
+import concourse.mybir as mybir
+
+F32 = mybir.dt.float32
+BF16 = mybir.dt.bfloat16
+I32 = mybir.dt.int32
+U32 = mybir.dt.uint32
+U16 = mybir.dt.uint16
+U8 = mybir.dt.uint8
+FP8X4 = mybir.dt.float8_e4m3fn_x4
+FP4X4 = mybir.dt.float4_e2m1fn_x4
+ALU = mybir.AluOpType
+ACT = mybir.ActivationFunctionType
+AX = mybir.AxisListType
+
+P = 128
+PACK = 4
+T = 2048
+SLOTS = 512
+ROWS = 128
+PAGES = 32
+PAGE = 16
+OUT_CHUNKS = (256, 512, 512, 512, 256)
+
+FLOPS = 2 * 2 * 512 * ROWS * SLOTS
+
+
+def tile_attend_bpagetimessigmoid_s_kernel(
+    tc, query, keys_words, keys_scales, th, sharp, gout, vals_words, vals_scales, old, offs, out
+):
+    nc = tc.nc
+    with ExitStack() as ctx:
+        sb = ctx.enter_context(tc.tile_pool(name="sb", bufs=1))
+        ps = ctx.enter_context(tc.psum_pool(name="ps", bufs=1))
+
+        def tile(name, shape, dtype, tag=None):
+            return sb.tile(shape, dtype, name=name, tag=tag or name, align_bytes=64)
+
+        offsets = sb.tile([P, SLOTS // 16], U16, name="offsets")
+        nc.sync.dma_start(offsets[:], offs)
+
+        def load_scale_rows(name, scales, queue):
+            plane = tile(name, [P, T], U8)
+            nc.vector.memset(plane[:].bitcast(I32), 0)
+            for quad in range(4):
+                queue.dma_start(
+                    plane[32 * quad : 32 * quad + 4, :].bitcast(I32),
+                    scales[0, 4 * quad : 4 * quad + 4, :].bitcast(I32),
+                )
+            return plane
+
+        def load_words(name, words, tag=None):
+            pool_words = tile(name, [P, T], U16, tag)
+            nc.sync.dma_start(pool_words[:].bitcast(I32), words[0].bitcast(I32))
+            return pool_words
+
+        def load_rows(name, src, tag=None):
+            raw = tile(name, [P, PACK, ROWS], F32, tag)
+            nc.sync.dma_start(raw[:], src.rearrange("(p j) w -> p j w", j=PACK))
+            return raw
+
+        def load_column(name, src, tag=None):
+            col = tile(name, [P, 1], F32, tag)
+            nc.sync.dma_start(col[:], src)
+            return col
+
+        def gather(name, window, dtype, tag=None):
+            picked = tile(name, [P, SLOTS], dtype, tag)
+            nc.vector.tensor_copy(picked[:], window[:].indirect(offsets[:]))
+            return picked
+
+        def interleave(name, raw):
+            grouped = tile(name, [P, ROWS, PACK], BF16)
+            nc.scalar.activation(grouped[:], raw[:].rearrange("p j w -> p w j"), ACT.Copy)
+            return grouped
+
+        def quantise(name, grouped):
+            codes = tile(name + "_codes", [P, ROWS], U32)
+            scales = tile(name + "_scales", [P, ROWS], U8)
+            nc.vector.quantize_mx(
+                out=codes[:].bitcast(FP8X4),
+                scales=scales[:],
+                in_=grouped[:].rearrange("p w j -> p (w j)"),
+            )
+            return codes, scales
+
+        def product(name, codes, scales, words, word_scales):
+            bank = ps.tile([ROWS, SLOTS], F32, name=name)
+            nc.tensor.matmul_mx(
+                out=bank[:],
+                lhsT=codes[:].bitcast(FP8X4),
+                lhsT_scale=scales[:],
+                rhs=words[:].bitcast(FP4X4),
+                rhs_scale=word_scales[:],
+                start=True,
+                stop=True,
+            )
+            return bank
+
+        def paged(ap):
+            return ap.rearrange("p (g i) -> p g i", i=PAGE)
+
+        def spread(ap):
+            return ap.unsqueeze(2).to_broadcast([P, PAGES, PAGE])
+
+        key_words = load_words("key_words", keys_words)
+        key_plane = load_scale_rows("key_plane", keys_scales, nc.sync)
+        q_raw = load_rows("q_raw", query)
+        g_raw = load_rows("g_raw", gout)
+        val_words = load_words("val_words", vals_words)
+        val_plane = load_scale_rows("val_plane", vals_scales, nc.sync)
+        th_col = load_column("th_col", th)
+        sharp_col = load_column("sharp_col", sharp)
+        total = tile("total", [P, T], F32)
+        nc.sync.dma_start(total[:], old)
+        placed = tile("placed", [P, T], F32)
+        nc.vector.memset(placed[:], 0.0)
+
+        key_word_cols = gather("key_word_cols", key_words, U16)
+        key_scale_cols = gather("key_scale_cols", key_plane, U8)
+        q_grouped = interleave("q_grouped", q_raw)
+        g_grouped = interleave("g_grouped", g_raw)
+        q_codes, q_scales = quantise("q", q_grouped)
+        a = product("a", q_codes, q_scales, key_word_cols, key_scale_cols)
+
+        val_word_cols = gather("val_word_cols", val_words, U16, "q_grouped")
+        g_codes, g_scales = quantise("g", g_grouped)
+        val_scale_cols = gather("val_scale_cols", val_plane, U8)
+        c0 = product("c0", g_codes, g_scales, val_word_cols, val_scale_cols)
+
+        gate_bias = tile("gate_bias", [P, 1], F32)
+        nc.scalar.mul(gate_bias[:], th_col[:], -0.5)
+        tanh_a = tile("tanh_a", [P, SLOTS], F32)
+        nc.scalar.activation(tanh_a[:], a[:], ACT.Tanh, bias=gate_bias[:], scale=0.5)
+        neg_mean_scale = tile("neg_mean_scale", [P, 1], F32)
+        nc.scalar.mul(neg_mean_scale[:], sharp_col[:], -1.0 / PAGE)
+
+        gate = tile("gate", [P, SLOTS], F32)
+        nc.scalar.activation(gate[:], tanh_a[:], ACT.Identity, bias=sharp_col[:], scale=sharp_col[:])
+
+        page_sum = tile("page_sum", [P, PAGES], F32, "val_plane")
+        nc.vector.tensor_reduce(page_sum[:], paged(a[:]), AX.X, ALU.add)
+        neg_s = tile("neg_s", [P, PAGES], F32)
+        neg_max = tile("neg_max", [P, 1], F32)
+        nc.vector.tensor_scalar(
+            neg_s[:], page_sum[:], neg_mean_scale[:], None, ALU.mult, ALU.min, accum_out=neg_max[:]
+        )
+        p = tile("p", [P, PAGES], F32)
+        z = tile("z", [P, 1], F32)
+        nc.scalar.activation(p[:], neg_s[:], ACT.Exp, bias=neg_max[:], scale=-1.0, accum_out=z[:])
+        tanh_sq8 = tile("tanh_sq8", [P, SLOTS], F32)
+        nc.scalar.activation(tanh_sq8[:], tanh_a[:], ACT.Square, scale=math.sqrt(8.0))
+
+        gated = tile("gated", [P, SLOTS], F32)
+        d_page = tile("d_page", [P, PAGES], F32)
+        neg_direct = tile("neg_direct", [P, SLOTS], F32)
+        halves = [slice(0, SLOTS // 2), slice(SLOTS // 2, SLOTS)]
+        page_halves = [slice(0, PAGES // 2), slice(PAGES // 2, PAGES)]
+        for h in halves:
+            nc.vector.tensor_tensor(gated[:, h], c0[:, h], gate[:, h], ALU.mult)
+        inv_z = tile("inv_z", [P, 1], F32)
+        nc.vector.reciprocal(inv_z[:], z[:])
+        share = tile("share", [P, SLOTS], F32)
+        nc.scalar.activation(paged(share[:]), spread(p[:]), ACT.Copy, scale=inv_z[:])
+        for h, g in zip(halves, page_halves):
+            nc.vector.tensor_reduce(d_page[:, g], paged(gated[:, h]), AX.X, ALU.add)
+
+        def direct_term(h):
+            nc.vector.scalar_tensor_tensor(
+                neg_direct[:, h], tanh_sq8[:, h], -8.0, c0[:, h], ALU.add, ALU.mult
+            )
+
+        direct_term(halves[0])
+        weighted = tile("weighted", [P, PAGES], F32)
+        d_mean = tile("d_mean", [P, 1], F32)
+        nc.vector.scalar_tensor_tensor(
+            weighted[:], d_page[:], inv_z[:], p[:], ALU.mult, ALU.mult, accum_out=d_mean[:]
+        )
+        direct_term(halves[1])
+        inner = tile("inner", [P, SLOTS], F32)
+        nc.vector.scalar_tensor_tensor(
+            paged(inner[:]), spread(d_page[:]), d_mean[:], paged(neg_direct[:]), ALU.subtract, ALU.subtract
+        )
+        nc.vector.tensor_tensor(placed[:].indirect(offsets[:]), inner[:], share[:], ALU.mult)
+
+        start = 0
+        for width in OUT_CHUNKS:
+            cols = slice(start, start + width)
+            nc.vector.tensor_tensor(total[:, cols], total[:, cols], placed[:, cols], ALU.add)
+            nc.sync.dma_start(out[:, cols], total[:, cols])
+            start = start + width

@@ -22,7 +22,7 @@ SLOTS = 512
 ROWS = 128
 PAGES = 32
 PAGE = 16
-OUT_CHUNKS = (256, 512, 512, 512, 256)
+OUT_CHUNKS = (256, 256, 384, 384, 384, 384)
 
 FLOPS = 2 * 2 * 512 * ROWS * SLOTS
 
@@ -44,10 +44,10 @@ def tile_attend_bpagetimessigmoid_s_kernel(
         def load_scale_rows(name, scales, queue):
             plane = tile(name, [P, T], U8)
             nc.vector.memset(plane[:].bitcast(I32), 0)
-            for quad in range(4):
+            for r in range(4):
                 queue.dma_start(
-                    plane[32 * quad : 32 * quad + 4, :].bitcast(I32),
-                    scales[0, 4 * quad : 4 * quad + 4, :].bitcast(I32),
+                    plane[r:P:32, :].bitcast(I32),
+                    scales[0, r:16:4, :].bitcast(I32),
                 )
             return plane
 
@@ -103,18 +103,16 @@ def tile_attend_bpagetimessigmoid_s_kernel(
             return ap.rearrange("p (g i) -> p g i", i=PAGE)
 
         def spread(ap):
-            return ap.unsqueeze(2).to_broadcast([P, PAGES, PAGE])
+            return ap.unsqueeze(2).to_broadcast([P, ap.shape[1], PAGE])
 
         key_words = load_words("key_words", keys_words)
         key_plane = load_scale_rows("key_plane", keys_scales, nc.sync)
         q_raw = load_rows("q_raw", query)
-        g_raw = load_rows("g_raw", gout)
         val_words = load_words("val_words", vals_words)
+        g_raw = load_rows("g_raw", gout)
         val_plane = load_scale_rows("val_plane", vals_scales, nc.sync)
         th_col = load_column("th_col", th)
         sharp_col = load_column("sharp_col", sharp)
-        total = tile("total", [P, T], F32)
-        nc.sync.dma_start(total[:], old)
         placed = tile("placed", [P, T], F32)
         nc.vector.memset(placed[:], 0.0)
 
@@ -126,6 +124,8 @@ def tile_attend_bpagetimessigmoid_s_kernel(
         a = product("a", q_codes, q_scales, key_word_cols, key_scale_cols)
 
         val_word_cols = gather("val_word_cols", val_words, U16, "q_grouped")
+        total = tile("total", [P, T], F32, "val_words")
+        nc.sync.dma_start(total[:], old)
         g_codes, g_scales = quantise("g", g_grouped)
         val_scale_cols = gather("val_scale_cols", val_plane, U8)
         c0 = product("c0", g_codes, g_scales, val_word_cols, val_scale_cols)
@@ -180,9 +180,11 @@ def tile_attend_bpagetimessigmoid_s_kernel(
         )
         direct_term(halves[1])
         inner = tile("inner", [P, SLOTS], F32)
-        nc.vector.scalar_tensor_tensor(
-            paged(inner[:]), spread(d_page[:]), d_mean[:], paged(neg_direct[:]), ALU.subtract, ALU.subtract
-        )
+        for h, g in zip(halves, page_halves):
+            nc.vector.scalar_tensor_tensor(
+                paged(inner[:, h]), spread(d_page[:, g]), d_mean[:], paged(neg_direct[:, h]),
+                ALU.subtract, ALU.subtract,
+            )
         nc.vector.tensor_tensor(placed[:].indirect(offsets[:]), inner[:], share[:], ALU.mult)
 
         start = 0

@@ -66,9 +66,9 @@ def tile_attend_bpagetimessigmoid_s_kernel(
             nc.sync.dma_start(col[:], src)
             return col
 
-        def gather(name, window, dtype, tag=None):
-            picked = tile(name, [P, SLOTS], dtype, tag)
-            nc.vector.tensor_copy(picked[:], window[:].indirect(offsets[:]))
+        def gather(name, window, dtype, tag=None, pages=slice(0, PAGES)):
+            picked = tile(name, [P, (pages.stop - pages.start) * PAGE], dtype, tag)
+            nc.vector.tensor_copy(picked[:], window[:].indirect(offsets[:, pages]))
             return picked
 
         def interleave(name, raw):
@@ -87,12 +87,12 @@ def tile_attend_bpagetimessigmoid_s_kernel(
             return codes, scales
 
         def product(name, codes, scales, words, word_scales):
-            bank = ps.tile([ROWS, SLOTS], F32, name=name)
+            bank = ps.tile([ROWS, words.shape[1]], F32, name=name)
             nc.tensor.matmul_mx(
                 out=bank[:],
                 lhsT=codes[:].bitcast(FP8X4),
                 lhsT_scale=scales[:],
-                rhs=words[:].bitcast(FP4X4),
+                rhs=words.bitcast(FP4X4),
                 rhs_scale=word_scales[:],
                 start=True,
                 stop=True,
@@ -105,12 +105,15 @@ def tile_attend_bpagetimessigmoid_s_kernel(
         def spread(ap):
             return ap.unsqueeze(2).to_broadcast([P, ap.shape[1], PAGE])
 
+        halves = [slice(0, SLOTS // 2), slice(SLOTS // 2, SLOTS)]
+        page_halves = [slice(0, PAGES // 2), slice(PAGES // 2, PAGES)]
+
         key_words = load_words("key_words", keys_words)
         key_plane = load_scale_rows("key_plane", keys_scales, nc.sync)
         q_raw = load_rows("q_raw", query)
         val_words = load_words("val_words", vals_words)
-        g_raw = load_rows("g_raw", gout)
         val_plane = load_scale_rows("val_plane", vals_scales, nc.sync)
+        g_raw = load_rows("g_raw", gout)
         th_col = load_column("th_col", th)
         sharp_col = load_column("sharp_col", sharp)
         placed = tile("placed", [P, T], F32)
@@ -121,14 +124,18 @@ def tile_attend_bpagetimessigmoid_s_kernel(
         q_grouped = interleave("q_grouped", q_raw)
         g_grouped = interleave("g_grouped", g_raw)
         q_codes, q_scales = quantise("q", q_grouped)
-        a = product("a", q_codes, q_scales, key_word_cols, key_scale_cols)
+        a = product("a", q_codes, q_scales, key_word_cols[:], key_scale_cols)
 
-        val_word_cols = gather("val_word_cols", val_words, U16, "q_grouped")
+        val_word_cols = gather("val_word_cols", val_words, U16, "q_raw")
         total = tile("total", [P, T], F32, "val_words")
         nc.sync.dma_start(total[:], old)
+        scales_lo = gather("val_scale_lo", val_plane, U8, None, page_halves[0])
         g_codes, g_scales = quantise("g", g_grouped)
-        val_scale_cols = gather("val_scale_cols", val_plane, U8)
-        c0 = product("c0", g_codes, g_scales, val_word_cols, val_scale_cols)
+        scales_hi = gather("val_scale_hi", val_plane, U8, "g_raw", page_halves[1])
+        c0 = [
+            product("c0_lo", g_codes, g_scales, val_word_cols[:, halves[0]], scales_lo),
+            product("c0_hi", g_codes, g_scales, val_word_cols[:, halves[1]], scales_hi),
+        ]
 
         gate_bias = tile("gate_bias", [P, 1], F32)
         nc.scalar.mul(gate_bias[:], th_col[:], -0.5)
@@ -140,9 +147,11 @@ def tile_attend_bpagetimessigmoid_s_kernel(
         gate = tile("gate", [P, SLOTS], F32)
         nc.scalar.activation(gate[:], tanh_a[:], ACT.Identity, bias=sharp_col[:], scale=sharp_col[:])
 
-        page_sum = tile("page_sum", [P, PAGES], F32, "val_plane")
+        page_sum = tile("page_sum", [P, PAGES], F32, "g_grouped")
         nc.vector.tensor_reduce(page_sum[:], paged(a[:]), AX.X, ALU.add)
-        neg_s = tile("neg_s", [P, PAGES], F32)
+        gated = tile("gated", [P, SLOTS], F32)
+        nc.vector.tensor_tensor(gated[:, halves[0]], c0[0][:], gate[:, halves[0]], ALU.mult)
+        neg_s = tile("neg_s", [P, PAGES], F32, "val_scale_lo")
         neg_max = tile("neg_max", [P, 1], F32)
         nc.vector.tensor_scalar(
             neg_s[:], page_sum[:], neg_mean_scale[:], None, ALU.mult, ALU.min, accum_out=neg_max[:]
@@ -153,13 +162,9 @@ def tile_attend_bpagetimessigmoid_s_kernel(
         tanh_sq8 = tile("tanh_sq8", [P, SLOTS], F32)
         nc.scalar.activation(tanh_sq8[:], tanh_a[:], ACT.Square, scale=math.sqrt(8.0))
 
-        gated = tile("gated", [P, SLOTS], F32)
         d_page = tile("d_page", [P, PAGES], F32)
         neg_direct = tile("neg_direct", [P, SLOTS], F32)
-        halves = [slice(0, SLOTS // 2), slice(SLOTS // 2, SLOTS)]
-        page_halves = [slice(0, PAGES // 2), slice(PAGES // 2, PAGES)]
-        for h in halves:
-            nc.vector.tensor_tensor(gated[:, h], c0[:, h], gate[:, h], ALU.mult)
+        nc.vector.tensor_tensor(gated[:, halves[1]], c0[1][:], gate[:, halves[1]], ALU.mult)
         inv_z = tile("inv_z", [P, 1], F32)
         nc.vector.reciprocal(inv_z[:], z[:])
         share = tile("share", [P, SLOTS], F32)
@@ -167,18 +172,18 @@ def tile_attend_bpagetimessigmoid_s_kernel(
         for h, g in zip(halves, page_halves):
             nc.vector.tensor_reduce(d_page[:, g], paged(gated[:, h]), AX.X, ALU.add)
 
-        def direct_term(h):
+        def direct_term(i):
             nc.vector.scalar_tensor_tensor(
-                neg_direct[:, h], tanh_sq8[:, h], -8.0, c0[:, h], ALU.add, ALU.mult
+                neg_direct[:, halves[i]], tanh_sq8[:, halves[i]], -8.0, c0[i][:], ALU.add, ALU.mult
             )
 
-        direct_term(halves[0])
+        direct_term(0)
         weighted = tile("weighted", [P, PAGES], F32)
         d_mean = tile("d_mean", [P, 1], F32)
         nc.vector.scalar_tensor_tensor(
             weighted[:], d_page[:], inv_z[:], p[:], ALU.mult, ALU.mult, accum_out=d_mean[:]
         )
-        direct_term(halves[1])
+        direct_term(1)
         inner = tile("inner", [P, SLOTS], F32)
         for h, g in zip(halves, page_halves):
             nc.vector.scalar_tensor_tensor(

import math
from contextlib import ExitStack

import concourse.mybir as mybir

F32 = mybir.dt.float32
BF16 = mybir.dt.bfloat16
I32 = mybir.dt.int32
U32 = mybir.dt.uint32
U16 = mybir.dt.uint16
U8 = mybir.dt.uint8
FP8X4 = mybir.dt.float8_e4m3fn_x4
FP4X4 = mybir.dt.float4_e2m1fn_x4
ALU = mybir.AluOpType
ACT = mybir.ActivationFunctionType
AX = mybir.AxisListType

P = 128
PACK = 4
T = 2048
SLOTS = 512
ROWS = 128
PAGES = 32
PAGE = 16
OUT_CHUNKS = (256, 256, 384, 384, 384, 384)

FLOPS = 2 * 2 * 512 * ROWS * SLOTS


def tile_attend_bpagetimessigmoid_s_kernel(
    tc, query, keys_words, keys_scales, th, sharp, gout, vals_words, vals_scales, old, offs, out
):
    nc = tc.nc
    with ExitStack() as ctx:
        sb = ctx.enter_context(tc.tile_pool(name="sb", bufs=1))
        ps = ctx.enter_context(tc.psum_pool(name="ps", bufs=1))

        def tile(name, shape, dtype, tag=None):
            return sb.tile(shape, dtype, name=name, tag=tag or name, align_bytes=64)

        offsets = sb.tile([P, SLOTS // 16], U16, name="offsets")
        nc.sync.dma_start(offsets[:], offs)

        def load_scale_rows(name, scales, queue):
            plane = tile(name, [P, T], U8)
            nc.vector.memset(plane[:].bitcast(I32), 0)
            for r in range(4):
                queue.dma_start(
                    plane[r:P:32, :].bitcast(I32),
                    scales[0, r:16:4, :].bitcast(I32),
                )
            return plane

        def load_words(name, words, tag=None):
            pool_words = tile(name, [P, T], U16, tag)
            nc.sync.dma_start(pool_words[:].bitcast(I32), words[0].bitcast(I32))
            return pool_words

        def load_rows(name, src, tag=None):
            raw = tile(name, [P, PACK, ROWS], F32, tag)
            nc.sync.dma_start(raw[:], src.rearrange("(p j) w -> p j w", j=PACK))
            return raw

        def load_column(name, src, tag=None):
            col = tile(name, [P, 1], F32, tag)
            nc.sync.dma_start(col[:], src)
            return col

        def gather(name, window, dtype, tag=None, pages=slice(0, PAGES)):
            picked = tile(name, [P, (pages.stop - pages.start) * PAGE], dtype, tag)
            nc.vector.tensor_copy(picked[:], window[:].indirect(offsets[:, pages]))
            return picked

        def interleave(name, raw):
            grouped = tile(name, [P, ROWS, PACK], BF16)
            nc.scalar.activation(grouped[:], raw[:].rearrange("p j w -> p w j"), ACT.Copy)
            return grouped

        def quantise(name, grouped):
            codes = tile(name + "_codes", [P, ROWS], U32)
            scales = tile(name + "_scales", [P, ROWS], U8)
            nc.vector.quantize_mx(
                out=codes[:].bitcast(FP8X4),
                scales=scales[:],
                in_=grouped[:].rearrange("p w j -> p (w j)"),
            )
            return codes, scales

        def product(name, codes, scales, words, word_scales):
            bank = ps.tile([ROWS, words.shape[1]], F32, name=name)
            nc.tensor.matmul_mx(
                out=bank[:],
                lhsT=codes[:].bitcast(FP8X4),
                lhsT_scale=scales[:],
                rhs=words.bitcast(FP4X4),
                rhs_scale=word_scales[:],
                start=True,
                stop=True,
            )
            return bank

        def paged(ap):
            return ap.rearrange("p (g i) -> p g i", i=PAGE)

        def spread(ap):
            return ap.unsqueeze(2).to_broadcast([P, ap.shape[1], PAGE])

        halves = [slice(0, SLOTS // 2), slice(SLOTS // 2, SLOTS)]
        page_halves = [slice(0, PAGES // 2), slice(PAGES // 2, PAGES)]

        key_words = load_words("key_words", keys_words)
        key_plane = load_scale_rows("key_plane", keys_scales, nc.sync)
        q_raw = load_rows("q_raw", query)
        val_words = load_words("val_words", vals_words)
        val_plane = load_scale_rows("val_plane", vals_scales, nc.sync)
        g_raw = load_rows("g_raw", gout)
        th_col = load_column("th_col", th)
        sharp_col = load_column("sharp_col", sharp)
        placed = tile("placed", [P, T], F32)
        nc.vector.memset(placed[:], 0.0)

        key_word_cols = gather("key_word_cols", key_words, U16)
        key_scale_cols = gather("key_scale_cols", key_plane, U8)
        q_grouped = interleave("q_grouped", q_raw)
        g_grouped = interleave("g_grouped", g_raw)
        q_codes, q_scales = quantise("q", q_grouped)
        a = product("a", q_codes, q_scales, key_word_cols[:], key_scale_cols)

        val_word_cols = gather("val_word_cols", val_words, U16, "q_raw")
        total = tile("total", [P, T], F32, "val_words")
        nc.sync.dma_start(total[:], old)
        scales_lo = gather("val_scale_lo", val_plane, U8, None, page_halves[0])
        g_codes, g_scales = quantise("g", g_grouped)
        scales_hi = gather("val_scale_hi", val_plane, U8, "g_raw", page_halves[1])
        c0 = [
            product("c0_lo", g_codes, g_scales, val_word_cols[:, halves[0]], scales_lo),
            product("c0_hi", g_codes, g_scales, val_word_cols[:, halves[1]], scales_hi),
        ]

        gate_bias = tile("gate_bias", [P, 1], F32)
        nc.scalar.mul(gate_bias[:], th_col[:], -0.5)
        tanh_a = tile("tanh_a", [P, SLOTS], F32)
        nc.scalar.activation(tanh_a[:], a[:], ACT.Tanh, bias=gate_bias[:], scale=0.5)
        neg_mean_scale = tile("neg_mean_scale", [P, 1], F32)
        nc.scalar.mul(neg_mean_scale[:], sharp_col[:], -1.0 / PAGE)

        gate = tile("gate", [P, SLOTS], F32)
        nc.scalar.activation(gate[:], tanh_a[:], ACT.Identity, bias=sharp_col[:], scale=sharp_col[:])

        page_sum = tile("page_sum", [P, PAGES], F32, "g_grouped")
        nc.vector.tensor_reduce(page_sum[:], paged(a[:]), AX.X, ALU.add)
        gated = tile("gated", [P, SLOTS], F32)
        nc.vector.tensor_tensor(gated[:, halves[0]], c0[0][:], gate[:, halves[0]], ALU.mult)
        neg_s = tile("neg_s", [P, PAGES], F32, "val_scale_lo")
        neg_max = tile("neg_max", [P, 1], F32)
        nc.vector.tensor_scalar(
            neg_s[:], page_sum[:], neg_mean_scale[:], None, ALU.mult, ALU.min, accum_out=neg_max[:]
        )
        p = tile("p", [P, PAGES], F32)
        z = tile("z", [P, 1], F32)
        nc.scalar.activation(p[:], neg_s[:], ACT.Exp, bias=neg_max[:], scale=-1.0, accum_out=z[:])
        tanh_sq8 = tile("tanh_sq8", [P, SLOTS], F32)
        nc.scalar.activation(tanh_sq8[:], tanh_a[:], ACT.Square, scale=math.sqrt(8.0))

        d_page = tile("d_page", [P, PAGES], F32)
        neg_direct = tile("neg_direct", [P, SLOTS], F32)
        nc.vector.tensor_tensor(gated[:, halves[1]], c0[1][:], gate[:, halves[1]], ALU.mult)
        inv_z = tile("inv_z", [P, 1], F32)
        nc.vector.reciprocal(inv_z[:], z[:])
        share = tile("share", [P, SLOTS], F32)
        nc.scalar.activation(paged(share[:]), spread(p[:]), ACT.Copy, scale=inv_z[:])
        for h, g in zip(halves, page_halves):
            nc.vector.tensor_reduce(d_page[:, g], paged(gated[:, h]), AX.X, ALU.add)

        def direct_term(i):
            nc.vector.scalar_tensor_tensor(
                neg_direct[:, halves[i]], tanh_sq8[:, halves[i]], -8.0, c0[i][:], ALU.add, ALU.mult
            )

        direct_term(0)
        weighted = tile("weighted", [P, PAGES], F32)
        d_mean = tile("d_mean", [P, 1], F32)
        nc.vector.scalar_tensor_tensor(
            weighted[:], d_page[:], inv_z[:], p[:], ALU.mult, ALU.mult, accum_out=d_mean[:]
        )
        direct_term(1)
        inner = tile("inner", [P, SLOTS], F32)
        for h, g in zip(halves, page_halves):
            nc.vector.scalar_tensor_tensor(
                paged(inner[:, h]), spread(d_page[:, g]), d_mean[:], paged(neg_direct[:, h]),
                ALU.subtract, ALU.subtract,
            )
        nc.vector.tensor_tensor(placed[:].indirect(offsets[:]), inner[:], share[:], ALU.mult)

        start = 0
        for width in OUT_CHUNKS:
            cols = slice(start, start + width)
            nc.vector.tensor_tensor(total[:, cols], total[:, cols], placed[:, cols], ALU.add)
            nc.sync.dma_start(out[:, cols], total[:, cols])
            start = start + width
